import numpy as np
import ml_dtypes


def mxq(x, axis, fmt="e4m3"):
    dtype, down = {"e4m3": (ml_dtypes.float8_e4m3fn, 7), "e5m2": (ml_dtypes.float8_e5m2, 14)}[fmt]
    v = np.moveaxis(np.asarray(x, np.float32).astype(ml_dtypes.bfloat16).astype(np.float64), axis, -1)
    blocks = v.reshape(v.shape[:-1] + (-1, 32))
    amax = np.abs(blocks).max(-1, keepdims=True)
    byte = np.maximum(np.where(amax > 0, np.frexp(amax)[1] - 1 + 127, 0) - down, 1)
    scale = np.exp2(byte - 127.0)
    codes = (blocks / scale).astype(np.float32).astype(dtype).astype(np.float64)
    return np.moveaxis((codes * scale).reshape(v.shape), -1, axis)


WIDE = False


def mx_kscale(k):
    if not WIDE:
        return np.ones(k)
    levels = np.array([10, -10, 5, -5, 0])
    if k % 512:
        return np.exp2(np.random.permutation(np.resize(levels, k // 32))).repeat(32)
    a = np.empty((k // 512, 16))
    for p in range(k // 512):
        a[p, :8] = np.random.permutation(np.resize(levels, 8))
        for g in range(8):
            far = levels[np.abs(levels - a[p, g]) >= 10]
            a[p, g + 8] = far[np.random.randint(len(far))]
    return np.exp2(a.ravel()).repeat(32)


def f64(x):
    return np.asarray(x).astype(np.float64)


def striped(idx):
    return np.tile(idx.reshape(-1, 16).T, (8, 1)).astype(np.uint16)


def unstriped(offs):
    return offs[:16].T.reshape(-1).astype(np.int64)


def pack_weight(w):
    k, n = w.shape
    w = f64(np.asarray(w, np.float32).astype(ml_dtypes.bfloat16)).reshape(k // 32, 32, n)
    amax = np.abs(w).max(1)
    byte = np.clip(np.where(amax > 0, np.frexp(amax)[1] - 1 + 127 - 7, 1), 1, 254)
    scaled = (w * np.exp2(127.0 - byte)[:, None, :]).reshape(k, n).astype(np.float32)
    words = np.ascontiguousarray(scaled.reshape(k // 512, 128, 4, n).transpose(0, 1, 3, 2)).astype(ml_dtypes.float8_e4m3fn).view(np.uint8)
    return words, np.ascontiguousarray(byte.astype(np.uint8).reshape(k // 512, 16, n))


def unpack_weight(words, scales):
    g, p, n, _ = words.shape
    vals = np.ascontiguousarray(words).view(ml_dtypes.float8_e4m3fn).astype(np.float64) * np.repeat(np.exp2(scales.astype(np.float64) - 127.0), 8, axis=1)[..., None]
    return vals.transpose(0, 1, 3, 2).reshape(g * 512, n)


def silu(v):
    return v / (1.0 + np.exp(-np.maximum(v, -700.0)))


K, T, H, N = 1024, 512, 512, 256


def setup_inputs():
    n = np.random.standard_normal
    s = mx_kscale(K)[:, None]
    u = mx_kscale(H)
    packed_xT = pack_weight(n((K, T)) * s)
    packed_w2 = pack_weight(n((H, N)) / np.sqrt(3 * H) / u[:, None])
    packed_w3 = pack_weight(n((H, N)) / np.sqrt(3 * H) / u[:, None])
    packed_w4 = pack_weight(n((H, N)) / np.sqrt(3 * H) / u[:, None])
    return {
        "x_words": packed_xT[0],
        "x_scales": packed_xT[1],
        "w1": (n((K, H)) / np.sqrt(K) / s * u).astype(np.float32),
        "w2_words": packed_w2[0],
        "w2_scales": packed_w2[1],
        "w3_words": packed_w3[0],
        "w3_scales": packed_w3[1],
        "w4_words": packed_w4[0],
        "w4_scales": packed_w4[1],
        "pos1": striped(np.random.permutation(T)),
        "pos2": striped(np.random.permutation(T)),
        "pos3": striped(np.random.permutation(T)),
        "pos4": striped(np.random.permutation(T)),
    }


def reference(x_words, x_scales, w1, w2_words, w2_scales, w3_words, w3_scales, w4_words, w4_scales, pos1, pos2, pos3, pos4):
    xq = unpack_weight(x_words, x_scales)
    h = silu(mxq(f64(w1), 0, "e4m3").T @ xq)
    g0 = h[:, unstriped(pos1)]
    g1 = h[:, unstriped(pos2)]
    g2 = h[:, unstriped(pos3)]
    g3 = h[:, unstriped(pos4)]
    z1 = (g0 + g1 + g2 + g3) / 4
    z2 = np.maximum(np.maximum(np.maximum(g0, g1), g2), g3)
    z3 = np.minimum(np.minimum(np.minimum(g0, g1), g2), g3)
    return unpack_weight(w2_words, w2_scales).T @ mxq(z1, 0, "e4m3") + unpack_weight(w3_words, w3_scales).T @ mxq(z2, 0, "e4m3") + unpack_weight(w4_words, w4_scales).T @ mxq(z3, 0, "e4m3")

@@ -1,0 +1,214 @@
+from contextlib import ExitStack
+
+import concourse.mybir as mybir
+from concourse.masks import make_identity
+
+K, T, H, N = 1024, 512, 512, 256
+FLOPS = 2 * K * H * T + 3 * 2 * H * N * T
+
+F32 = mybir.dt.float32
+BF16 = mybir.dt.bfloat16
+I32 = mybir.dt.int32
+U32 = mybir.dt.uint32
+U16 = mybir.dt.uint16
+U8 = mybir.dt.uint8
+FP8X4 = mybir.dt.float8_e4m3fn_x4
+ACT = mybir.ActivationFunctionType
+ALU = mybir.AluOpType
+
+P = 128
+PACK = 4
+PASSES = K // (P * PACK)
+LISTS = 4
+WINDOW = 704
+HALF = T // 2
+HALVES = ((0, HALF), (HALF, HALF))
+CHUNKS = (((0, 256),), ((256, 128), (384, 128)))
+
+
+def tile_picked_wpna_silu_l_kernel(
+    tc, x_words, x_scales, w1, w2_words, w2_scales, w3_words, w3_scales, w4_words, w4_scales, pos1, pos2, pos3, pos4, out
+):
+    nc = tc.nc
+    with ExitStack() as ctx:
+        keep = ctx.enter_context(tc.tile_pool(name="keep", bufs=1))
+        psum = ctx.enter_context(tc.psum_pool(name="psum", bufs=1))
+
+        def load_scales(queue, plane, scales):
+            for q in range(4):
+                queue.dma_start(
+                    out=plane[32 * q : 32 * q + 4, :, :].bitcast(I32),
+                    in_=scales[:, 4 * q : 4 * q + 4, :].rearrange("g r n -> r g n").bitcast(I32),
+                )
+
+        def load_words(words, g, name):
+            tile = keep.tile([P, words.shape[2]], U32, name=name, align_bytes=64)
+            nc.sync.dma_start(out=tile[:].bitcast(I32), in_=words[g].rearrange("p n t -> p (n t)").bitcast(I32))
+            return tile
+
+        x_plane = keep.tile([P, PASSES, T], U8, name="x_plane", align_bytes=64)
+        nc.vector.memset(x_plane[:].bitcast(I32), 0)
+        load_scales(nc.scalar, x_plane, x_scales)
+        warm_in = keep.tile([P, 8], F32, name="warm_in")
+        warm_out = keep.tile([P, 8], F32, name="warm_out")
+        nc.vector.memset(warm_in[:], 0.0)
+        nc.scalar.activation(warm_out[:], warm_in[:], ACT.Silu)
+        w_planes = [keep.tile([P, 1, N], U8, name=f"w_plane{s}", align_bytes=64) for s in range(3)]
+        for plane in w_planes:
+            nc.gpsimd.memset(plane[:].bitcast(I32), 0)
+        h = [keep.tile([P, WINDOW], F32, name=f"h{t}") for t in range(PACK)]
+        for t in range(PACK):
+            nc.gpsimd.memset(h[t][:, T:], 0.0)
+        ident = keep.tile([P, P], F32, name="ident")
+        make_identity(nc, ident[:])
+
+        def load_w1(g, c0, n):
+            tile = keep.tile([P, PACK, n], F32, name=f"w1_raw{g}_{c0}")
+            rows = w1[g * P * PACK : (g + 1) * P * PACK, c0 : c0 + n]
+            nc.sync.dma_start(out=tile[:], in_=rows.rearrange("(p j) c -> p j c", j=PACK))
+            return (g, c0, n, tile)
+
+        pieces = [load_w1(0, 0, H), load_w1(1, 0, H // 2)]
+        xq = [load_words(x_words, 0, "xq0")]
+        pieces.append(load_w1(1, H // 2, H // 2))
+        xq.append(load_words(x_words, 1, "xq1"))
+        offs = []
+        for d, pos in enumerate((pos1, pos2, pos3, pos4)):
+            tile = keep.tile([P, T // 16], U16, name=f"offs{d}")
+            nc.sync.dma_start(tile[:], pos)
+            offs.append(tile)
+        wq2 = [load_words(w, 0, f"wq2_{s}") for s, w in enumerate((w2_words, w3_words, w4_words))]
+        for plane, scales in zip(w_planes, (w2_scales, w3_scales, w4_scales)):
+            load_scales(nc.sync, plane, scales)
+
+        grouped = [keep.tile([P, PACK, P, PACK], BF16, name=f"grouped{g}", align_bytes=64) for g in range(PASSES)]
+        w1_codes = [keep.tile([P, H], U32, name=f"w1_codes{g}", align_bytes=64) for g in range(PASSES)]
+        w1_plane = [keep.tile([P, H], U8, name=f"w1_plane{g}", align_bytes=64) for g in range(PASSES)]
+
+        def round_w1(g, c0, n, tile):
+            nc.vector.tensor_copy(
+                out=grouped[g][:, :, c0 // PACK : (c0 + n) // PACK, :].rearrange("p t m j -> p m t j"),
+                in_=tile[:].rearrange("p j (m t) -> p m t j", t=PACK),
+            )
+
+        def quantise_w1(g, t0, t1):
+            nc.vector.quantize_mx(
+                out=w1_codes[g][:, t0 * P : t1 * P].bitcast(FP8X4),
+                scales=w1_plane[g][:, t0 * P : t1 * P],
+                in_=grouped[g][:, t0:t1].rearrange("p t m j -> p (t m j)"),
+            )
+
+        acc = [psum.tile([P, T], F32, name=f"acc{t}", tag=f"bank{t}") for t in range(PACK)]
+
+        def first_product(g, t):
+            nc.tensor.matmul_mx(
+                out=acc[t][:],
+                lhsT=w1_codes[g][:, t * P : (t + 1) * P].bitcast(FP8X4),
+                lhsT_scale=w1_plane[g][:, t * P : (t + 1) * P],
+                rhs=xq[g][:].bitcast(FP8X4),
+                rhs_scale=x_plane[:, g, :],
+                start=(g == 0),
+                stop=(g == PASSES - 1),
+            )
+
+        round_w1(*pieces[0])
+        round_w1(*pieces[1])
+        quantise_w1(0, 0, PACK)
+        for t in range(PACK):
+            first_product(0, t)
+        round_w1(*pieces[2])
+        for t in range(PACK):
+            quantise_w1(1, t, t + 1)
+            first_product(1, t)
+            nc.scalar.activation(h[t][:, :T], acc[t][:], ACT.Silu)
+
+        sums = [psum.tile([P, PACK, P], F32, name=f"sums{b}", tag=f"bank{b}") for b in range(T // P)]
+        rounded = {}
+
+        def fetch(d, v0, n, parts):
+            got = keep.tile([P, PACK, n], F32, name=f"got{d}_{v0}")
+            for t in range(PACK):
+                nc.vector.tensor_copy(got[:, t, :], h[t][:].indirect(offs[d][:, v0 // 16 : (v0 + n) // 16]))
+                for b in range(n // P):
+                    nc.tensor.matmul(
+                        sums[v0 // P + b][:, t, :],
+                        got[:, t, b * P : (b + 1) * P],
+                        ident[:],
+                        start=(d == 0 and t == 0),
+                        stop=(d == LISTS - 1 and t == PACK - 1),
+                        is_transpose=True,
+                    )
+            for c0, m in parts:
+                tile = keep.tile([P, m * PACK], BF16, name=f"rounded{d}_{c0}", align_bytes=64)
+                nc.scalar.copy(
+                    out=tile[:].rearrange("p (c i t) -> p c t i", i=4, t=PACK),
+                    in_=got[:, :, c0 - v0 : c0 - v0 + m].rearrange("p t (c i) -> p c t i", i=4),
+                )
+                rounded[d, c0] = tile
+
+        def pair(op, name, a, b, width):
+            tile = keep.tile([P, width], BF16, name=name, align_bytes=64)
+            nc.vector.tensor_tensor(tile[:], a, b, op)
+            return tile
+
+        def mean(v0, n):
+            back = psum.tile([P, n // P, 2, P], F32, name=f"back{v0}", tag=f"back{(v0 // P) % 2}")
+            for b in range(n // P):
+                turned = keep.tile([P, 2, P, 2], BF16, name=f"turned{v0}_{b}")
+                nc.scalar.activation(
+                    turned[:], sums[v0 // P + b][:].rearrange("v (u e) p -> v u p e", e=2), ACT.Copy, scale=1.0 / LISTS
+                )
+                words = turned[:].rearrange("v u p e -> v (u p e)").bitcast(F32)
+                for u in range(2):
+                    nc.tensor.transpose(back[:, b, u, :], words[:, u * P : (u + 1) * P], ident[:])
+            tile = keep.tile([P, n * PACK], BF16, name=f"mean{v0}", align_bytes=64)
+            nc.scalar.copy(
+                out=tile[:].bitcast(F32).rearrange("p (b v u) -> p b v u", u=2, v=P),
+                in_=back[:].rearrange("p b u v -> p b v u"),
+            )
+            return tile
+
+        def second_product(v0, n, stats):
+            res = [psum.tile([P, n], F32, name=f"res{v0}_{m}", tag=f"res{m}") for m in range(N // P)]
+            for s, z in enumerate(stats):
+                codes = keep.tile([P, n], U32, name=f"z_codes{v0}_{s}", align_bytes=64)
+                plane = keep.tile([P, n], U8, name=f"z_plane{v0}_{s}", align_bytes=64)
+                nc.vector.quantize_mx(out=codes[:].bitcast(FP8X4), scales=plane[:], in_=z[:])
+                for m in range(N // P):
+                    nc.tensor.matmul_mx(
+                        out=res[m][:],
+                        lhsT=wq2[s][:, m * P : (m + 1) * P].bitcast(FP8X4),
+                        lhsT_scale=w_planes[s][:, 0, m * P : (m + 1) * P],
+                        rhs=codes[:].bitcast(FP8X4),
+                        rhs_scale=plane[:],
+                        start=(s == 0),
+                        stop=(s == 2),
+                    )
+            staged = keep.tile([P, N // P, n], F32, name=f"staged{v0}")
+            for m in range(N // P):
+                nc.scalar.copy(out=staged[:, m, :], in_=res[m][:])
+            nc.sync.dma_start(out=out[:, v0 : v0 + n].rearrange("(m p) v -> p m v", p=P), in_=staged[:])
+
+        fetch(0, 0, T, ((0, T),))
+        fetch(1, 0, T, ((0, T),))
+        means = {}
+        for (v0, n), chunks in zip(HALVES, CHUNKS):
+            fetch(2, v0, n, ((v0, n),))
+            fetch(3, v0, n, chunks)
+            for c0, m in chunks:
+                means[c0] = mean(c0, m)
+        ops = (ALU.max, ALU.min)
+        first = [pair(op, f"first{k}", rounded[0, 0][:], rounded[1, 0][:], T * PACK) for k, op in enumerate(ops)]
+        second = {}
+        for v0, n in HALVES:
+            cols = slice(v0 * PACK, (v0 + n) * PACK)
+            for k, op in enumerate(ops):
+                second[v0, k] = pair(op, f"second{v0}_{k}", first[k][:, cols], rounded[2, v0][:], n * PACK)
+        for (v0, n), chunks in zip(HALVES, CHUNKS):
+            for c0, m in chunks:
+                cols = slice((c0 - v0) * PACK, (c0 - v0 + m) * PACK)
+                third = [
+                    pair(op, f"third{c0}_{k}", second[v0, k][:, cols], rounded[3, c0][:], m * PACK)
+                    for k, op in enumerate(ops)
+                ]
+                second_product(c0, m, [means[c0]] + third)

@@ -21,6 +21,7 @@ PACK = 4
 PASSES = K // (P * PACK)
 LISTS = 4
 WINDOW = 704
+VECTOR_SHARE = 88
 HALF = T // 2
 HALVES = ((0, HALF), (HALF, HALF))
 CHUNKS = (((0, 256),), ((256, 128), (384, 128)))
@@ -62,16 +63,14 @@ def tile_picked_wpna_silu_l_kernel(
         ident = keep.tile([P, P], F32, name="ident")
         make_identity(nc, ident[:])
 
-        def load_w1(g, c0, n):
-            tile = keep.tile([P, PACK, n], F32, name=f"w1_raw{g}_{c0}")
-            rows = w1[g * P * PACK : (g + 1) * P * PACK, c0 : c0 + n]
+        def load_w1(g):
+            tile = keep.tile([P, PACK, H], F32, name=f"w1_raw{g}")
+            rows = w1[g * P * PACK : (g + 1) * P * PACK, :]
             nc.sync.dma_start(out=tile[:], in_=rows.rearrange("(p j) c -> p j c", j=PACK))
-            return (g, c0, n, tile)
+            return tile
 
-        pieces = [load_w1(0, 0, H), load_w1(1, 0, H // 2)]
-        xq = [load_words(x_words, 0, "xq0")]
-        pieces.append(load_w1(1, H // 2, H // 2))
-        xq.append(load_words(x_words, 1, "xq1"))
+        raw = [load_w1(g) for g in range(PASSES)]
+        xq = [load_words(x_words, g, f"xq{g}") for g in range(PASSES)]
         offs = []
         for d, pos in enumerate((pos1, pos2, pos3, pos4)):
             tile = keep.tile([P, T // 16], U16, name=f"offs{d}")
@@ -85,10 +84,10 @@ def tile_picked_wpna_silu_l_kernel(
         w1_codes = [keep.tile([P, H], U32, name=f"w1_codes{g}", align_bytes=64) for g in range(PASSES)]
         w1_plane = [keep.tile([P, H], U8, name=f"w1_plane{g}", align_bytes=64) for g in range(PASSES)]
 
-        def round_w1(g, c0, n, tile):
-            nc.vector.tensor_copy(
-                out=grouped[g][:, :, c0 // PACK : (c0 + n) // PACK, :].rearrange("p t m j -> p m t j"),
-                in_=tile[:].rearrange("p j (m t) -> p m t j", t=PACK),
+        def round_w1(copy, g, m0, m1):
+            copy(
+                out=grouped[g][:, :, m0:m1, :].rearrange("p t m j -> p m t j"),
+                in_=raw[g][:, :, m0 * PACK : m1 * PACK].rearrange("p j (m t) -> p m t j", t=PACK),
             )
 
         def quantise_w1(g, t0, t1):
@@ -111,14 +110,13 @@ def tile_picked_wpna_silu_l_kernel(
                 stop=(g == PASSES - 1),
             )
 
-        round_w1(*pieces[0])
-        round_w1(*pieces[1])
+        round_w1(nc.vector.tensor_copy, 0, 0, P)
         quantise_w1(0, 0, PACK)
-        for t in range(PACK):
-            first_product(0, t)
-        round_w1(*pieces[2])
+        round_w1(nc.vector.tensor_copy, 1, 0, VECTOR_SHARE)
+        round_w1(nc.scalar.copy, 1, VECTOR_SHARE, P)
         for t in range(PACK):
             quantise_w1(1, t, t + 1)
+            first_product(0, t)
             first_product(1, t)
             nc.scalar.activation(h[t][:, :T], acc[t][:], ACT.Silu)
 
@@ -168,9 +166,9 @@ def tile_picked_wpna_silu_l_kernel(
             )
             return tile
 
-        def second_product(v0, n, stats):
-            res = [psum.tile([P, n], F32, name=f"res{v0}_{m}", tag=f"res{m}") for m in range(N // P)]
-            for s, z in enumerate(stats):
+        def second_product(v0, n, stats, tag, copies):
+            res = [psum.tile([P, n], F32, name=f"res{v0}_{m}", tag=f"{tag}{m}") for m in range(N // P)]
+            for k, (s, z) in enumerate(stats):
                 codes = keep.tile([P, n], U32, name=f"z_codes{v0}_{s}", align_bytes=64)
                 plane = keep.tile([P, n], U8, name=f"z_plane{v0}_{s}", align_bytes=64)
                 nc.vector.quantize_mx(out=codes[:].bitcast(FP8X4), scales=plane[:], in_=z[:])
@@ -181,12 +179,12 @@ def tile_picked_wpna_silu_l_kernel(
                         lhsT_scale=w_planes[s][:, 0, m * P : (m + 1) * P],
                         rhs=codes[:].bitcast(FP8X4),
                         rhs_scale=plane[:],
-                        start=(s == 0),
-                        stop=(s == 2),
+                        start=(k == 0),
+                        stop=(k == 2),
                     )
             staged = keep.tile([P, N // P, n], F32, name=f"staged{v0}")
             for m in range(N // P):
-                nc.scalar.copy(out=staged[:, m, :], in_=res[m][:])
+                copies[m](out=staged[:, m, :], in_=res[m][:])
             nc.sync.dma_start(out=out[:, v0 : v0 + n].rearrange("(m p) v -> p m v", p=P), in_=staged[:])
 
         fetch(0, 0, T, ((0, T),))
@@ -211,4 +209,7 @@ def tile_picked_wpna_silu_l_kernel(
                     pair(op, f"third{c0}_{k}", second[v0, k][:, cols], rounded[3, c0][:], m * PACK)
                     for k, op in enumerate(ops)
                 ]
-                second_product(c0, m, [means[c0]] + third)
+                last = c0 + m == T
+                copies = (nc.scalar.copy, nc.vector.tensor_copy if last else nc.scalar.copy)
+                tag = "bank" if c0 == HALF else "res"
+                second_product(c0, m, [(1, third[0]), (2, third[1]), (0, means[c0])], tag, copies)

@@ -20,11 +20,9 @@ P = 128
 PACK = 4
 PASSES = K // (P * PACK)
 LISTS = 4
-WINDOW = 704
+SPARE = 192
 VECTOR_SHARE = 88
 HALF = T // 2
-HALVES = ((0, HALF), (HALF, HALF))
-CHUNKS = (((0, 256),), ((256, 128), (384, 128)))
 
 
 def tile_picked_wpna_silu_l_kernel(
@@ -48,8 +46,7 @@ def tile_picked_wpna_silu_l_kernel(
             return tile
 
         x_plane = keep.tile([P, PASSES, T], U8, name="x_plane", align_bytes=64)
-        nc.vector.memset(x_plane[:].bitcast(I32), 0)
-        load_scales(nc.scalar, x_plane, x_scales)
+        nc.gpsimd.memset(x_plane[:].bitcast(I32), 0)
         warm_in = keep.tile([P, 8], F32, name="warm_in")
         warm_out = keep.tile([P, 8], F32, name="warm_out")
         nc.vector.memset(warm_in[:], 0.0)
@@ -57,20 +54,23 @@ def tile_picked_wpna_silu_l_kernel(
         w_planes = [keep.tile([P, 1, N], U8, name=f"w_plane{s}", align_bytes=64) for s in range(3)]
         for plane in w_planes:
             nc.gpsimd.memset(plane[:].bitcast(I32), 0)
-        h = [keep.tile([P, WINDOW], F32, name=f"h{t}") for t in range(PACK)]
-        for t in range(PACK):
-            nc.gpsimd.memset(h[t][:, T:], 0.0)
+        h = keep.tile([P, PACK * T + SPARE], F32, name="h")
+        nc.gpsimd.memset(h[:, PACK * T :], 0.0)
         ident = keep.tile([P, P], F32, name="ident")
         make_identity(nc, ident[:])
 
-        def load_w1(g):
-            tile = keep.tile([P, PACK, H], F32, name=f"w1_raw{g}")
-            rows = w1[g * P * PACK : (g + 1) * P * PACK, :]
-            nc.sync.dma_start(out=tile[:], in_=rows.rearrange("(p j) c -> p j c", j=PACK))
+        def load_w1(g, j0, rows):
+            tile = keep.tile([P, rows, H], F32, name=f"w1_raw{g}_{j0}")
+            src = w1[g * P * PACK : (g + 1) * P * PACK, :].rearrange("(p j) c -> p j c", j=PACK)
+            nc.sync.dma_start(out=tile[:], in_=src[:, j0 : j0 + rows, :])
             return tile
 
-        raw = [load_w1(g) for g in range(PASSES)]
-        xq = [load_words(x_words, g, f"xq{g}") for g in range(PASSES)]
+        raw = {(0, 0): load_w1(0, 0, PACK)}
+        load_scales(nc.sync, x_plane, x_scales)
+        xq = [load_words(x_words, 0, "xq0")]
+        for j0 in (0, 2):
+            raw[1, j0] = load_w1(1, j0, 2)
+        xq.append(load_words(x_words, 1, "xq1"))
         offs = []
         for d, pos in enumerate((pos1, pos2, pos3, pos4)):
             tile = keep.tile([P, T // 16], U16, name=f"offs{d}")
@@ -84,10 +84,10 @@ def tile_picked_wpna_silu_l_kernel(
         w1_codes = [keep.tile([P, H], U32, name=f"w1_codes{g}", align_bytes=64) for g in range(PASSES)]
         w1_plane = [keep.tile([P, H], U8, name=f"w1_plane{g}", align_bytes=64) for g in range(PASSES)]
 
-        def round_w1(copy, g, m0, m1):
+        def round_w1(copy, g, j0, rows, m0, m1):
             copy(
-                out=grouped[g][:, :, m0:m1, :].rearrange("p t m j -> p m t j"),
-                in_=raw[g][:, :, m0 * PACK : m1 * PACK].rearrange("p j (m t) -> p m t j", t=PACK),
+                out=grouped[g][:, :, m0:m1, j0 : j0 + rows].rearrange("p t m j -> p m t j"),
+                in_=raw[g, j0][:, :, m0 * PACK : m1 * PACK].rearrange("p j (m t) -> p m t j", t=PACK),
             )
 
         def quantise_w1(g, t0, t1):
@@ -110,15 +110,18 @@ def tile_picked_wpna_silu_l_kernel(
                 stop=(g == PASSES - 1),
             )
 
-        round_w1(nc.vector.tensor_copy, 0, 0, P)
-        quantise_w1(0, 0, PACK)
-        round_w1(nc.vector.tensor_copy, 1, 0, VECTOR_SHARE)
-        round_w1(nc.scalar.copy, 1, VECTOR_SHARE, P)
+        round_w1(nc.vector.tensor_copy, 0, 0, PACK, 0, VECTOR_SHARE)
+        round_w1(nc.scalar.copy, 0, 0, PACK, VECTOR_SHARE, P)
+        for t in range(PACK):
+            quantise_w1(0, t, t + 1)
+            first_product(0, t)
+        round_w1(nc.vector.tensor_copy, 1, 0, 2, 0, P)
+        round_w1(nc.vector.tensor_copy, 1, 2, 2, 0, VECTOR_SHARE)
+        round_w1(nc.scalar.copy, 1, 2, 2, VECTOR_SHARE, P)
         for t in range(PACK):
             quantise_w1(1, t, t + 1)
-            first_product(0, t)
             first_product(1, t)
-            nc.scalar.activation(h[t][:, :T], acc[t][:], ACT.Silu)
+            nc.scalar.activation(h[:, t * T : (t + 1) * T], acc[t][:], ACT.Silu)
 
         sums = [psum.tile([P, PACK, P], F32, name=f"sums{b}", tag=f"bank{b}") for b in range(T // P)]
         rounded = {}
@@ -126,7 +129,13 @@ def tile_picked_wpna_silu_l_kernel(
         def fetch(d, v0, n, parts):
             got = keep.tile([P, PACK, n], F32, name=f"got{d}_{v0}")
             for t in range(PACK):
-                nc.vector.tensor_copy(got[:, t, :], h[t][:].indirect(offs[d][:, v0 // 16 : (v0 + n) // 16]))
+                if d == 0 and t < PACK - 1:
+                    window, step = h[:, t * T : (t + 1) * T], HALF
+                else:
+                    window, step = h[:, t * T : min(t * T + PACK * T, PACK * T + SPARE)], n
+                for s0 in range(0, n, step):
+                    entries = offs[d][:, (v0 + s0) // 16 : (v0 + s0 + step) // 16]
+                    nc.vector.tensor_copy(got[:, t, s0 : s0 + step], window.indirect(entries))
                 for b in range(n // P):
                     nc.tensor.matmul(
                         sums[v0 // P + b][:, t, :],
@@ -144,13 +153,13 @@ def tile_picked_wpna_silu_l_kernel(
                 )
                 rounded[d, c0] = tile
 
-        def pair(op, name, a, b, width):
-            tile = keep.tile([P, width], BF16, name=name, align_bytes=64)
+        def pair(op, name, a, b, width, slot=None):
+            tile = keep.tile([P, width], BF16, name=name, tag=slot or name, align_bytes=64)
             nc.vector.tensor_tensor(tile[:], a, b, op)
             return tile
 
-        def mean(v0, n):
-            back = psum.tile([P, n // P, 2, P], F32, name=f"back{v0}", tag=f"back{(v0 // P) % 2}")
+        def turn_back(v0, n, bank):
+            back = psum.tile([P, n // P, 2, P], F32, name=f"back{v0}", tag=bank)
             for b in range(n // P):
                 turned = keep.tile([P, 2, P, 2], BF16, name=f"turned{v0}_{b}")
                 nc.scalar.activation(
@@ -159,57 +168,77 @@ def tile_picked_wpna_silu_l_kernel(
                 words = turned[:].rearrange("v u p e -> v (u p e)").bitcast(F32)
                 for u in range(2):
                     nc.tensor.transpose(back[:, b, u, :], words[:, u * P : (u + 1) * P], ident[:])
-            tile = keep.tile([P, n * PACK], BF16, name=f"mean{v0}", align_bytes=64)
+            return back
+
+        def mean(back, v0, n):
+            tile = keep.tile([P, n * PACK], BF16, name=f"mean{v0}", tag=f"mean{v0}", align_bytes=64)
             nc.scalar.copy(
                 out=tile[:].bitcast(F32).rearrange("p (b v u) -> p b v u", u=2, v=P),
                 in_=back[:].rearrange("p b u v -> p b v u"),
             )
             return tile
 
-        def second_product(v0, n, stats, tag, copies):
-            res = [psum.tile([P, n], F32, name=f"res{v0}_{m}", tag=f"{tag}{m}") for m in range(N // P)]
-            for k, (s, z) in enumerate(stats):
-                codes = keep.tile([P, n], U32, name=f"z_codes{v0}_{s}", align_bytes=64)
-                plane = keep.tile([P, n], U8, name=f"z_plane{v0}_{s}", align_bytes=64)
-                nc.vector.quantize_mx(out=codes[:].bitcast(FP8X4), scales=plane[:], in_=z[:])
-                for m in range(N // P):
-                    nc.tensor.matmul_mx(
-                        out=res[m][:],
-                        lhsT=wq2[s][:, m * P : (m + 1) * P].bitcast(FP8X4),
-                        lhsT_scale=w_planes[s][:, 0, m * P : (m + 1) * P],
-                        rhs=codes[:].bitcast(FP8X4),
-                        rhs_scale=plane[:],
-                        start=(k == 0),
-                        stop=(k == 2),
-                    )
+        def quantise(name, z):
+            n = z.shape[1] // PACK
+            codes = keep.tile([P, n], U32, name=f"{name}_codes", align_bytes=64)
+            plane = keep.tile([P, n], U8, name=f"{name}_plane", align_bytes=64)
+            nc.vector.quantize_mx(out=codes[:].bitcast(FP8X4), scales=plane[:], in_=z)
+            return codes[:], plane[:]
+
+        def results(v0, n, banks):
+            return [psum.tile([P, n], F32, name=f"res{v0}_{m}", tag=banks[m]) for m in range(N // P)]
+
+        def second_product(res, s, z, start=False, stop=False):
+            for m in range(N // P):
+                nc.tensor.matmul_mx(
+                    out=res[m][:],
+                    lhsT=wq2[s][:, m * P : (m + 1) * P].bitcast(FP8X4),
+                    lhsT_scale=w_planes[s][:, 0, m * P : (m + 1) * P],
+                    rhs=z[0].bitcast(FP8X4),
+                    rhs_scale=z[1],
+                    start=start,
+                    stop=stop,
+                )
+
+        def store(res, v0, n, copies):
             staged = keep.tile([P, N // P, n], F32, name=f"staged{v0}")
             for m in range(N // P):
                 copies[m](out=staged[:, m, :], in_=res[m][:])
             nc.sync.dma_start(out=out[:, v0 : v0 + n].rearrange("(m p) v -> p m v", p=P), in_=staged[:])
 
-        fetch(0, 0, T, ((0, T),))
-        fetch(1, 0, T, ((0, T),))
-        means = {}
-        for (v0, n), chunks in zip(HALVES, CHUNKS):
-            fetch(2, v0, n, ((v0, n),))
-            fetch(3, v0, n, chunks)
-            for c0, m in chunks:
-                means[c0] = mean(c0, m)
+        for d in range(LISTS - 1):
+            fetch(d, 0, T, ((0, T),))
+        fetch(3, 0, HALF, ((0, HALF),))
+        back = turn_back(0, HALF, "back0")
+        fetch(3, HALF, HALF, ((HALF, HALF),))
+        mean_a = mean(back, 0, HALF)
+        quarters = (HALF, HALF + P)
+        backs = [turn_back(v0, P, bank) for v0, bank in zip(quarters, ("back1", "bank2"))]
+        means_b = [mean(back, v0, P) for v0, back in zip(quarters, backs)]
+
         ops = (ALU.max, ALU.min)
         first = [pair(op, f"first{k}", rounded[0, 0][:], rounded[1, 0][:], T * PACK) for k, op in enumerate(ops)]
-        second = {}
-        for v0, n in HALVES:
-            cols = slice(v0 * PACK, (v0 + n) * PACK)
-            for k, op in enumerate(ops):
-                second[v0, k] = pair(op, f"second{v0}_{k}", first[k][:, cols], rounded[2, v0][:], n * PACK)
-        for (v0, n), chunks in zip(HALVES, CHUNKS):
-            for c0, m in chunks:
-                cols = slice((c0 - v0) * PACK, (c0 - v0 + m) * PACK)
-                third = [
-                    pair(op, f"third{c0}_{k}", second[v0, k][:, cols], rounded[3, c0][:], m * PACK)
-                    for k, op in enumerate(ops)
-                ]
-                last = c0 + m == T
-                copies = (nc.scalar.copy, nc.vector.tensor_copy if last else nc.scalar.copy)
-                tag = "bank" if c0 == HALF else "res"
-                second_product(c0, m, [(1, third[0]), (2, third[1]), (0, means[c0])], tag, copies)
+        second = [pair(op, f"second{k}", first[k][:], rounded[2, 0][:], T * PACK) for k, op in enumerate(ops)]
+
+        width = HALF * PACK
+        third = [pair(op, f"third_a{k}", second[k][:, :width], rounded[3, 0][:], width) for k, op in enumerate(ops)]
+        res = results(0, HALF, ("bank2", "back1"))
+        second_product(res, 1, quantise("max_a", third[0][:]), start=True)
+        second_product(res, 2, quantise("min_a", third[1][:]))
+        second_product(res, 0, quantise("mean_a", mean_a[:]), stop=True)
+        store(res, 0, HALF, (nc.scalar.copy, nc.scalar.copy))
+
+        res = [results(v0, P, banks) for v0, banks in zip(quarters, (("bank0", "bank1"), ("bank3", "back0")))]
+        for q in range(2):
+            second_product(res[q], 0, quantise(f"mean_b{q}", means_b[q][:]), start=True)
+        third = [
+            pair(op, f"third_b{k}", second[k][:, width:], rounded[3, HALF][:], width, f"mean{quarters[k]}")
+            for k, op in enumerate(ops)
+        ]
+        codes, plane = quantise("max_b", third[0][:])
+        for q in range(2):
+            second_product(res[q], 1, (codes[:, q * P : (q + 1) * P], plane[:, q * P : (q + 1) * P]))
+        for q in range(2):
+            z = third[1][:, q * P * PACK : (q + 1) * P * PACK]
+            second_product(res[q], 2, quantise(f"min_b{q}", z), stop=True)
+            store(res[q], quarters[q], P, (nc.scalar.copy, nc.vector.tensor_copy if q else nc.scalar.copy))

@@ -21,7 +21,6 @@ PACK = 4
 PASSES = K // (P * PACK)
 LISTS = 4
 SPARE = 192
-VECTOR_SHARE = 88
 HALF = T // 2
 
 
@@ -65,7 +64,7 @@ def tile_picked_wpna_silu_l_kernel(
             nc.sync.dma_start(out=tile[:], in_=src[:, j0 : j0 + rows, :])
             return tile
 
-        raw = {(0, 0): load_w1(0, 0, PACK)}
+        raw = {(0, j0): load_w1(0, j0, 2) for j0 in (0, 2)}
         load_scales(nc.sync, x_plane, x_scales)
         xq = [load_words(x_words, 0, "xq0")]
         for j0 in (0, 2):
@@ -84,10 +83,10 @@ def tile_picked_wpna_silu_l_kernel(
         w1_codes = [keep.tile([P, H], U32, name=f"w1_codes{g}", align_bytes=64) for g in range(PASSES)]
         w1_plane = [keep.tile([P, H], U8, name=f"w1_plane{g}", align_bytes=64) for g in range(PASSES)]
 
-        def round_w1(copy, g, j0, rows, m0, m1):
+        def round_w1(copy, g, j0, rows, ms, ts):
             copy(
-                out=grouped[g][:, :, m0:m1, j0 : j0 + rows].rearrange("p t m j -> p m t j"),
-                in_=raw[g, j0][:, :, m0 * PACK : m1 * PACK].rearrange("p j (m t) -> p m t j", t=PACK),
+                out=grouped[g][:, ts, ms, j0 : j0 + rows].rearrange("p t m j -> p m t j"),
+                in_=raw[g, j0][:].rearrange("p j (m t) -> p m t j", t=PACK)[:, ms, ts, :],
             )
 
         def quantise_w1(g, t0, t1):
@@ -110,18 +109,17 @@ def tile_picked_wpna_silu_l_kernel(
                 stop=(g == PASSES - 1),
             )
 
-        round_w1(nc.vector.tensor_copy, 0, 0, PACK, 0, VECTOR_SHARE)
-        round_w1(nc.scalar.copy, 0, 0, PACK, VECTOR_SHARE, P)
-        for t in range(PACK):
-            quantise_w1(0, t, t + 1)
-            first_product(0, t)
-        round_w1(nc.vector.tensor_copy, 1, 0, 2, 0, P)
-        round_w1(nc.vector.tensor_copy, 1, 2, 2, 0, VECTOR_SHARE)
-        round_w1(nc.scalar.copy, 1, 2, 2, VECTOR_SHARE, P)
-        for t in range(PACK):
-            quantise_w1(1, t, t + 1)
-            first_product(1, t)
-            nc.scalar.activation(h[:, t * T : (t + 1) * T], acc[t][:], ACT.Silu)
+        every = slice(None)
+        for g in range(PASSES):
+            round_w1(nc.vector.tensor_copy, g, 0, 2, every, every)
+            round_w1(nc.scalar.copy, g, 2, 2, every, slice(2, 4))
+            for t in range(PACK):
+                if t < 2:
+                    round_w1(nc.vector.tensor_copy, g, 2, 2, every, slice(t, t + 1))
+                quantise_w1(g, t, t + 1)
+                first_product(g, t)
+                if g == PASSES - 1:
+                    nc.scalar.activation(h[:, t * T : (t + 1) * T], acc[t][:], ACT.Silu)
 
         sums = [psum.tile([P, PACK, P], F32, name=f"sums{b}", tag=f"bank{b}") for b in range(T // P)]
         rounded = {}
@@ -200,17 +198,25 @@ def tile_picked_wpna_silu_l_kernel(
                     stop=stop,
                 )
 
-        def store(res, v0, n, copies):
+        def store(res, v0, n):
             staged = keep.tile([P, N // P, n], F32, name=f"staged{v0}")
             for m in range(N // P):
-                copies[m](out=staged[:, m, :], in_=res[m][:])
+                nc.scalar.copy(out=staged[:, m, :], in_=res[m][:])
             nc.sync.dma_start(out=out[:, v0 : v0 + n].rearrange("(m p) v -> p m v", p=P), in_=staged[:])
 
-        for d in range(LISTS - 1):
+        def store_last(res, v0, n):
+            for m, (copy, queue) in enumerate(((nc.scalar.copy, nc.scalar), (nc.vector.tensor_copy, nc.sync))):
+                staged = keep.tile([P, n], F32, name=f"staged{v0}_{m}")
+                copy(out=staged[:], in_=res[m][:])
+                queue.dma_start(out=out[m * P : (m + 1) * P, v0 : v0 + n], in_=staged[:])
+
+        for d in (0, 1):
             fetch(d, 0, T, ((0, T),))
-        fetch(3, 0, HALF, ((0, HALF),))
+        for d in (2, 3):
+            fetch(d, 0, HALF, ((0, HALF),))
         back = turn_back(0, HALF, "back0")
-        fetch(3, HALF, HALF, ((HALF, HALF),))
+        for d in (2, 3):
+            fetch(d, HALF, HALF, ((HALF, HALF),))
         mean_a = mean(back, 0, HALF)
         quarters = (HALF, HALF + P)
         backs = [turn_back(v0, P, bank) for v0, bank in zip(quarters, ("back1", "bank2"))]
@@ -218,21 +224,22 @@ def tile_picked_wpna_silu_l_kernel(
 
         ops = (ALU.max, ALU.min)
         first = [pair(op, f"first{k}", rounded[0, 0][:], rounded[1, 0][:], T * PACK) for k, op in enumerate(ops)]
-        second = [pair(op, f"second{k}", first[k][:], rounded[2, 0][:], T * PACK) for k, op in enumerate(ops)]
 
         width = HALF * PACK
-        third = [pair(op, f"third_a{k}", second[k][:, :width], rounded[3, 0][:], width) for k, op in enumerate(ops)]
+        second = [pair(op, f"second_a{k}", first[k][:, :width], rounded[2, 0][:], width) for k, op in enumerate(ops)]
+        third = [pair(op, f"third_a{k}", second[k][:], rounded[3, 0][:], width) for k, op in enumerate(ops)]
         res = results(0, HALF, ("bank2", "back1"))
         second_product(res, 1, quantise("max_a", third[0][:]), start=True)
         second_product(res, 2, quantise("min_a", third[1][:]))
         second_product(res, 0, quantise("mean_a", mean_a[:]), stop=True)
-        store(res, 0, HALF, (nc.scalar.copy, nc.scalar.copy))
+        store(res, 0, HALF)
 
+        second = [pair(op, f"second_b{k}", first[k][:, width:], rounded[2, HALF][:], width) for k, op in enumerate(ops)]
         res = [results(v0, P, banks) for v0, banks in zip(quarters, (("bank0", "bank1"), ("bank3", "back0")))]
         for q in range(2):
             second_product(res[q], 0, quantise(f"mean_b{q}", means_b[q][:]), start=True)
         third = [
-            pair(op, f"third_b{k}", second[k][:, width:], rounded[3, HALF][:], width, f"mean{quarters[k]}")
+            pair(op, f"third_b{k}", second[k][:], rounded[3, HALF][:], width, f"mean{quarters[k]}")
             for k, op in enumerate(ops)
         ]
         codes, plane = quantise("max_b", third[0][:])
@@ -241,4 +248,4 @@ def tile_picked_wpna_silu_l_kernel(
         for q in range(2):
             z = third[1][:, q * P * PACK : (q + 1) * P * PACK]
             second_product(res[q], 2, quantise(f"min_b{q}", z), stop=True)
-            store(res[q], quarters[q], P, (nc.scalar.copy, nc.vector.tensor_copy if q else nc.scalar.copy))
+            (store, store_last)[q](res[q], quarters[q], P)

@@ -198,25 +198,17 @@ def tile_picked_wpna_silu_l_kernel(
                     stop=stop,
                 )
 
-        def store(res, v0, n):
+        def store(res, v0, n, copies):
             staged = keep.tile([P, N // P, n], F32, name=f"staged{v0}")
             for m in range(N // P):
-                nc.scalar.copy(out=staged[:, m, :], in_=res[m][:])
+                copies[m](out=staged[:, m, :], in_=res[m][:])
             nc.sync.dma_start(out=out[:, v0 : v0 + n].rearrange("(m p) v -> p m v", p=P), in_=staged[:])
 
-        def store_last(res, v0, n):
-            for m, (copy, queue) in enumerate(((nc.scalar.copy, nc.scalar), (nc.vector.tensor_copy, nc.sync))):
-                staged = keep.tile([P, n], F32, name=f"staged{v0}_{m}")
-                copy(out=staged[:], in_=res[m][:])
-                queue.dma_start(out=out[m * P : (m + 1) * P, v0 : v0 + n], in_=staged[:])
-
-        for d in (0, 1):
+        for d in range(LISTS - 1):
             fetch(d, 0, T, ((0, T),))
-        for d in (2, 3):
-            fetch(d, 0, HALF, ((0, HALF),))
+        fetch(3, 0, HALF, ((0, HALF),))
         back = turn_back(0, HALF, "back0")
-        for d in (2, 3):
-            fetch(d, HALF, HALF, ((HALF, HALF),))
+        fetch(3, HALF, HALF, ((HALF, HALF),))
         mean_a = mean(back, 0, HALF)
         quarters = (HALF, HALF + P)
         backs = [turn_back(v0, P, bank) for v0, bank in zip(quarters, ("back1", "bank2"))]
@@ -224,22 +216,21 @@ def tile_picked_wpna_silu_l_kernel(
 
         ops = (ALU.max, ALU.min)
         first = [pair(op, f"first{k}", rounded[0, 0][:], rounded[1, 0][:], T * PACK) for k, op in enumerate(ops)]
+        second = [pair(op, f"second{k}", first[k][:], rounded[2, 0][:], T * PACK) for k, op in enumerate(ops)]
 
         width = HALF * PACK
-        second = [pair(op, f"second_a{k}", first[k][:, :width], rounded[2, 0][:], width) for k, op in enumerate(ops)]
-        third = [pair(op, f"third_a{k}", second[k][:], rounded[3, 0][:], width) for k, op in enumerate(ops)]
+        third = [pair(op, f"third_a{k}", second[k][:, :width], rounded[3, 0][:], width) for k, op in enumerate(ops)]
         res = results(0, HALF, ("bank2", "back1"))
         second_product(res, 1, quantise("max_a", third[0][:]), start=True)
         second_product(res, 2, quantise("min_a", third[1][:]))
         second_product(res, 0, quantise("mean_a", mean_a[:]), stop=True)
-        store(res, 0, HALF)
+        store(res, 0, HALF, (nc.scalar.copy, nc.scalar.copy))
 
-        second = [pair(op, f"second_b{k}", first[k][:, width:], rounded[2, HALF][:], width) for k, op in enumerate(ops)]
         res = [results(v0, P, banks) for v0, banks in zip(quarters, (("bank0", "bank1"), ("bank3", "back0")))]
         for q in range(2):
             second_product(res[q], 0, quantise(f"mean_b{q}", means_b[q][:]), start=True)
         third = [
-            pair(op, f"third_b{k}", second[k][:], rounded[3, HALF][:], width, f"mean{quarters[k]}")
+            pair(op, f"third_b{k}", second[k][:, width:], rounded[3, HALF][:], width, f"mean{quarters[k]}")
             for k, op in enumerate(ops)
         ]
         codes, plane = quantise("max_b", third[0][:])
@@ -248,4 +239,4 @@ def tile_picked_wpna_silu_l_kernel(
         for q in range(2):
             z = third[1][:, q * P * PACK : (q + 1) * P * PACK]
             second_product(res[q], 2, quantise(f"min_b{q}", z), stop=True)
-            (store, store_last)[q](res[q], quarters[q], P)
+            store(res[q], quarters[q], P, (nc.scalar.copy, nc.vector.tensor_copy if q else nc.scalar.copy))

from contextlib import ExitStack

import concourse.mybir as mybir
from concourse.masks import make_identity

K, T, H, N = 1024, 512, 512, 256
FLOPS = 2 * K * H * T + 3 * 2 * H * N * T

F32 = mybir.dt.float32
BF16 = mybir.dt.bfloat16
I32 = mybir.dt.int32
U32 = mybir.dt.uint32
U16 = mybir.dt.uint16
U8 = mybir.dt.uint8
FP8X4 = mybir.dt.float8_e4m3fn_x4
ACT = mybir.ActivationFunctionType
ALU = mybir.AluOpType

P = 128
PACK = 4
PASSES = K // (P * PACK)
LISTS = 4
SPARE = 192
HALF = T // 2


def tile_picked_wpna_silu_l_kernel(
    tc, x_words, x_scales, w1, w2_words, w2_scales, w3_words, w3_scales, w4_words, w4_scales, pos1, pos2, pos3, pos4, out
):
    nc = tc.nc
    with ExitStack() as ctx:
        keep = ctx.enter_context(tc.tile_pool(name="keep", bufs=1))
        psum = ctx.enter_context(tc.psum_pool(name="psum", bufs=1))

        def load_scales(queue, plane, scales):
            for q in range(4):
                queue.dma_start(
                    out=plane[32 * q : 32 * q + 4, :, :].bitcast(I32),
                    in_=scales[:, 4 * q : 4 * q + 4, :].rearrange("g r n -> r g n").bitcast(I32),
                )

        def load_words(words, g, name):
            tile = keep.tile([P, words.shape[2]], U32, name=name, align_bytes=64)
            nc.sync.dma_start(out=tile[:].bitcast(I32), in_=words[g].rearrange("p n t -> p (n t)").bitcast(I32))
            return tile

        x_plane = keep.tile([P, PASSES, T], U8, name="x_plane", align_bytes=64)
        nc.gpsimd.memset(x_plane[:].bitcast(I32), 0)
        warm_in = keep.tile([P, 8], F32, name="warm_in")
        warm_out = keep.tile([P, 8], F32, name="warm_out")
        nc.vector.memset(warm_in[:], 0.0)
        nc.scalar.activation(warm_out[:], warm_in[:], ACT.Silu)
        w_planes = [keep.tile([P, 1, N], U8, name=f"w_plane{s}", align_bytes=64) for s in range(3)]
        for plane in w_planes:
            nc.gpsimd.memset(plane[:].bitcast(I32), 0)
        h = keep.tile([P, PACK * T + SPARE], F32, name="h")
        nc.gpsimd.memset(h[:, PACK * T :], 0.0)
        ident = keep.tile([P, P], F32, name="ident")
        make_identity(nc, ident[:])

        def load_w1(g, j0, rows):
            tile = keep.tile([P, rows, H], F32, name=f"w1_raw{g}_{j0}")
            src = w1[g * P * PACK : (g + 1) * P * PACK, :].rearrange("(p j) c -> p j c", j=PACK)
            nc.sync.dma_start(out=tile[:], in_=src[:, j0 : j0 + rows, :])
            return tile

        raw = {(0, j0): load_w1(0, j0, 2) for j0 in (0, 2)}
        load_scales(nc.sync, x_plane, x_scales)
        xq = [load_words(x_words, 0, "xq0")]
        for j0 in (0, 2):
            raw[1, j0] = load_w1(1, j0, 2)
        xq.append(load_words(x_words, 1, "xq1"))
        offs = []
        for d, pos in enumerate((pos1, pos2, pos3, pos4)):
            tile = keep.tile([P, T // 16], U16, name=f"offs{d}")
            nc.sync.dma_start(tile[:], pos)
            offs.append(tile)
        wq2 = [load_words(w, 0, f"wq2_{s}") for s, w in enumerate((w2_words, w3_words, w4_words))]
        for plane, scales in zip(w_planes, (w2_scales, w3_scales, w4_scales)):
            load_scales(nc.sync, plane, scales)

        grouped = [keep.tile([P, PACK, P, PACK], BF16, name=f"grouped{g}", align_bytes=64) for g in range(PASSES)]
        w1_codes = [keep.tile([P, H], U32, name=f"w1_codes{g}", align_bytes=64) for g in range(PASSES)]
        w1_plane = [keep.tile([P, H], U8, name=f"w1_plane{g}", align_bytes=64) for g in range(PASSES)]

        def round_w1(copy, g, j0, rows, ms, ts):
            copy(
                out=grouped[g][:, ts, ms, j0 : j0 + rows].rearrange("p t m j -> p m t j"),
                in_=raw[g, j0][:].rearrange("p j (m t) -> p m t j", t=PACK)[:, ms, ts, :],
            )

        def quantise_w1(g, t0, t1):
            nc.vector.quantize_mx(
                out=w1_codes[g][:, t0 * P : t1 * P].bitcast(FP8X4),
                scales=w1_plane[g][:, t0 * P : t1 * P],
                in_=grouped[g][:, t0:t1].rearrange("p t m j -> p (t m j)"),
            )

        acc = [psum.tile([P, T], F32, name=f"acc{t}", tag=f"bank{t}") for t in range(PACK)]

        def first_product(g, t):
            nc.tensor.matmul_mx(
                out=acc[t][:],
                lhsT=w1_codes[g][:, t * P : (t + 1) * P].bitcast(FP8X4),
                lhsT_scale=w1_plane[g][:, t * P : (t + 1) * P],
                rhs=xq[g][:].bitcast(FP8X4),
                rhs_scale=x_plane[:, g, :],
                start=(g == 0),
                stop=(g == PASSES - 1),
            )

        every = slice(None)
        for g in range(PASSES):
            round_w1(nc.vector.tensor_copy, g, 0, 2, every, every)
            round_w1(nc.scalar.copy, g, 2, 2, every, slice(2, 4))
            for t in range(PACK):
                if t < 2:
                    round_w1(nc.vector.tensor_copy, g, 2, 2, every, slice(t, t + 1))
                quantise_w1(g, t, t + 1)
                first_product(g, t)
                if g == PASSES - 1:
                    nc.scalar.activation(h[:, t * T : (t + 1) * T], acc[t][:], ACT.Silu)

        sums = [psum.tile([P, PACK, P], F32, name=f"sums{b}", tag=f"bank{b}") for b in range(T // P)]
        rounded = {}

        def fetch(d, v0, n, parts):
            got = keep.tile([P, PACK, n], F32, name=f"got{d}_{v0}")
            for t in range(PACK):
                if d == 0 and t < PACK - 1:
                    window, step = h[:, t * T : (t + 1) * T], HALF
                else:
                    window, step = h[:, t * T : min(t * T + PACK * T, PACK * T + SPARE)], n
                for s0 in range(0, n, step):
                    entries = offs[d][:, (v0 + s0) // 16 : (v0 + s0 + step) // 16]
                    nc.vector.tensor_copy(got[:, t, s0 : s0 + step], window.indirect(entries))
                for b in range(n // P):
                    nc.tensor.matmul(
                        sums[v0 // P + b][:, t, :],
                        got[:, t, b * P : (b + 1) * P],
                        ident[:],
                        start=(d == 0 and t == 0),
                        stop=(d == LISTS - 1 and t == PACK - 1),
                        is_transpose=True,
                    )
            for c0, m in parts:
                tile = keep.tile([P, m * PACK], BF16, name=f"rounded{d}_{c0}", align_bytes=64)
                nc.scalar.copy(
                    out=tile[:].rearrange("p (c i t) -> p c t i", i=4, t=PACK),
                    in_=got[:, :, c0 - v0 : c0 - v0 + m].rearrange("p t (c i) -> p c t i", i=4),
                )
                rounded[d, c0] = tile

        def pair(op, name, a, b, width, slot=None):
            tile = keep.tile([P, width], BF16, name=name, tag=slot or name, align_bytes=64)
            nc.vector.tensor_tensor(tile[:], a, b, op)
            return tile

        def turn_back(v0, n, bank):
            back = psum.tile([P, n // P, 2, P], F32, name=f"back{v0}", tag=bank)
            for b in range(n // P):
                turned = keep.tile([P, 2, P, 2], BF16, name=f"turned{v0}_{b}")
                nc.scalar.activation(
                    turned[:], sums[v0 // P + b][:].rearrange("v (u e) p -> v u p e", e=2), ACT.Copy, scale=1.0 / LISTS
                )
                words = turned[:].rearrange("v u p e -> v (u p e)").bitcast(F32)
                for u in range(2):
                    nc.tensor.transpose(back[:, b, u, :], words[:, u * P : (u + 1) * P], ident[:])
            return back

        def mean(back, v0, n):
            tile = keep.tile([P, n * PACK], BF16, name=f"mean{v0}", tag=f"mean{v0}", align_bytes=64)
            nc.scalar.copy(
                out=tile[:].bitcast(F32).rearrange("p (b v u) -> p b v u", u=2, v=P),
                in_=back[:].rearrange("p b u v -> p b v u"),
            )
            return tile

        def quantise(name, z):
            n = z.shape[1] // PACK
            codes = keep.tile([P, n], U32, name=f"{name}_codes", align_bytes=64)
            plane = keep.tile([P, n], U8, name=f"{name}_plane", align_bytes=64)
            nc.vector.quantize_mx(out=codes[:].bitcast(FP8X4), scales=plane[:], in_=z)
            return codes[:], plane[:]

        def results(v0, n, banks):
            return [psum.tile([P, n], F32, name=f"res{v0}_{m}", tag=banks[m]) for m in range(N // P)]

        def second_product(res, s, z, start=False, stop=False):
            for m in range(N // P):
                nc.tensor.matmul_mx(
                    out=res[m][:],
                    lhsT=wq2[s][:, m * P : (m + 1) * P].bitcast(FP8X4),
                    lhsT_scale=w_planes[s][:, 0, m * P : (m + 1) * P],
                    rhs=z[0].bitcast(FP8X4),
                    rhs_scale=z[1],
                    start=start,
                    stop=stop,
                )

        def store(res, v0, n, copies):
            staged = keep.tile([P, N // P, n], F32, name=f"staged{v0}")
            for m in range(N // P):
                copies[m](out=staged[:, m, :], in_=res[m][:])
            nc.sync.dma_start(out=out[:, v0 : v0 + n].rearrange("(m p) v -> p m v", p=P), in_=staged[:])

        for d in range(LISTS - 1):
            fetch(d, 0, T, ((0, T),))
        fetch(3, 0, HALF, ((0, HALF),))
        back = turn_back(0, HALF, "back0")
        fetch(3, HALF, HALF, ((HALF, HALF),))
        mean_a = mean(back, 0, HALF)
        quarters = (HALF, HALF + P)
        backs = [turn_back(v0, P, bank) for v0, bank in zip(quarters, ("back1", "bank2"))]
        means_b = [mean(back, v0, P) for v0, back in zip(quarters, backs)]

        ops = (ALU.max, ALU.min)
        first = [pair(op, f"first{k}", rounded[0, 0][:], rounded[1, 0][:], T * PACK) for k, op in enumerate(ops)]
        second = [pair(op, f"second{k}", first[k][:], rounded[2, 0][:], T * PACK) for k, op in enumerate(ops)]

        width = HALF * PACK
        third = [pair(op, f"third_a{k}", second[k][:, :width], rounded[3, 0][:], width) for k, op in enumerate(ops)]
        res = results(0, HALF, ("bank2", "back1"))
        second_product(res, 1, quantise("max_a", third[0][:]), start=True)
        second_product(res, 2, quantise("min_a", third[1][:]))
        second_product(res, 0, quantise("mean_a", mean_a[:]), stop=True)
        store(res, 0, HALF, (nc.scalar.copy, nc.scalar.copy))

        res = [results(v0, P, banks) for v0, banks in zip(quarters, (("bank0", "bank1"), ("bank3", "back0")))]
        for q in range(2):
            second_product(res[q], 0, quantise(f"mean_b{q}", means_b[q][:]), start=True)
        third = [
            pair(op, f"third_b{k}", second[k][:, width:], rounded[3, HALF][:], width, f"mean{quarters[k]}")
            for k, op in enumerate(ops)
        ]
        codes, plane = quantise("max_b", third[0][:])
        for q in range(2):
            second_product(res[q], 1, (codes[:, q * P : (q + 1) * P], plane[:, q * P : (q + 1) * P]))
        for q in range(2):
            z = third[1][:, q * P * PACK : (q + 1) * P * PACK]
            second_product(res[q], 2, quantise(f"min_b{q}", z), stop=True)
            store(res[q], quarters[q], P, (nc.scalar.copy, nc.vector.tensor_copy if q else nc.scalar.copy))
